import numpy as np
import ml_dtypes


def mxq(x, axis, fmt="e4m3"):
    dtype, down = {"e4m3": (ml_dtypes.float8_e4m3fn, 7), "e5m2": (ml_dtypes.float8_e5m2, 14)}[fmt]
    v = np.moveaxis(np.asarray(x, np.float32).astype(ml_dtypes.bfloat16).astype(np.float64), axis, -1)
    blocks = v.reshape(v.shape[:-1] + (-1, 32))
    amax = np.abs(blocks).max(-1, keepdims=True)
    byte = np.maximum(np.where(amax > 0, np.frexp(amax)[1] - 1 + 127, 0) - down, 1)
    scale = np.exp2(byte - 127.0)
    codes = (blocks / scale).astype(np.float32).astype(dtype).astype(np.float64)
    return np.moveaxis((codes * scale).reshape(v.shape), -1, axis)


WIDE = False


def mx_kscale(k):
    if not WIDE:
        return np.ones(k)
    levels = np.array([10, -10, 5, -5, 0])
    if k % 512:
        return np.exp2(np.random.permutation(np.resize(levels, k // 32))).repeat(32)
    a = np.empty((k // 512, 16))
    for p in range(k // 512):
        a[p, :8] = np.random.permutation(np.resize(levels, 8))
        for g in range(8):
            far = levels[np.abs(levels - a[p, g]) >= 10]
            a[p, g + 8] = far[np.random.randint(len(far))]
    return np.exp2(a.ravel()).repeat(32)


def f64(x):
    return np.asarray(x).astype(np.float64)


def striped(idx):
    return np.tile(np.asarray(idx).reshape(-1, 16).T, (8, 1)).astype(np.uint16)


def unstriped(offs):
    return offs[:16].T.reshape(-1).astype(np.int64)


E2M1 = np.array([0.0, 0.5, 1.0, 1.5, 2.0, 3.0, 4.0, 6.0, -0.0, -0.5, -1.0, -1.5, -2.0, -3.0, -4.0, -6.0])


def pack_weight(w, fmt):
    k, n = w.shape
    w = f64(np.asarray(w, np.float32).astype(ml_dtypes.bfloat16)).reshape(k // 32, 32, n)
    amax = np.abs(w).max(1)
    if fmt == "e4m3":
        byte = np.frexp(amax)[1] - 1 + 127 - 7
    else:
        mant, ex = np.frexp(amax / 6.0)
        byte = np.where(mant > 0.5, ex, ex - 1) + 127
    byte = np.clip(np.where(amax > 0, byte, 1), 1, 254)
    scaled = (w * np.exp2(127.0 - byte)[:, None, :]).reshape(k, n).astype(np.float32)
    by_word = np.ascontiguousarray(scaled.reshape(k // 512, 128, 4, n).transpose(0, 1, 3, 2))
    if fmt == "e4m3":
        words = by_word.astype(ml_dtypes.float8_e4m3fn).view(np.uint8)
    else:
        c = by_word.astype(ml_dtypes.float4_e2m1fn).view(np.uint8) & 0xF
        words = (c[..., 0::2] | (c[..., 1::2] << 4)).reshape(k // 512, 128, 2 * n)
    return np.ascontiguousarray(words), np.ascontiguousarray(byte.astype(np.uint8).reshape(k // 512, 16, n))


def unpack_weight(words, scales, fmt):
    g, _, n = scales.shape
    words = np.ascontiguousarray(words).reshape(g, 128, n, -1)
    if fmt == "e4m3":
        vals = words.view(ml_dtypes.float8_e4m3fn).astype(np.float64)
    else:
        nib = np.empty((g, 128, n, 4), np.uint8)
        nib[..., 0::2] = words & 0xF
        nib[..., 1::2] = words >> 4
        vals = E2M1[nib]
    vals = vals * np.repeat(np.exp2(scales.astype(np.float64) - 127.0), 8, axis=1)[..., None]
    return vals.transpose(0, 1, 3, 2).reshape(g * 512, n)


D, T, I, Q, E, J, U = 512, 2048, 512, 128, 512, 256, 1024


def setup_inputs():
    n = np.random.standard_normal
    idx = np.random.permutation(T)[:I]
    idx2 = np.random.permutation(U)[:J]
    fd = mx_kscale(D)
    fi = mx_kscale(I)
    ti = np.ones(T)
    ti[idx] = fi
    keysp = pack_weight(n((D, T)) / fd[:, None], "e4m3")
    return {
        "query": (n((D, Q)) * 0.8 / np.sqrt(D) * fd[:, None]).astype(np.float32),
        "keys_words": keysp[0],
        "keys_scales": keysp[1],
        "kept": (n((D, U)) * 1.5 / np.sqrt(D) * fd[:, None]).astype(np.float32),
        "kw1": (np.random.uniform(0.4, 1.6, (1, J))).astype(np.float32),
        "lam": (np.random.uniform(0.3, 0.7, (1, Q))).astype(np.float32),
        "os": (np.random.uniform(4.0, 16.0, (1, I)) * fi).astype(np.float32),
        "vals": (n((E, T)) / ti).astype(np.float32),
        "offs": striped(idx),
        "offs2": striped(idx2),
    }


def reference(query, keys_words, keys_scales, kept, kw1, lam, os, vals, offs, offs2):
    idx = unstriped(offs)
    idx2 = unstriped(offs2)
    keysu = unpack_weight(keys_words, keys_scales, "e4m3")
    keysidxg = keysu[:, idx]
    queryq = mxq(f64(query), 0, "e4m3")
    a0 = keysidxg.T @ queryq
    keptidx2q = mxq(f64(kept)[:, idx2], 0, "e4m3")
    kk = keysidxg.T @ keptidx2q
    m1 = np.max(kk * f64(kw1), axis=1, keepdims=True)
    s0 = a0 - m1 * f64(lam)
    s = s0.T
    p = np.exp(s - np.max(s, axis=1, keepdims=True))
    w = p / np.sum(p, axis=1, keepdims=True)
    wo1 = w * f64(os)
    wt1 = wo1.T
    vt1 = f64(vals)[:, idx].T
    wt1q = mxq(wt1, 0, "e4m3")
    vt1q = mxq(vt1, 0, "e4m3")
    o = wt1q.T @ vt1q
    return o

@@ -1,0 +1,180 @@
+from contextlib import ExitStack
+
+import concourse.mybir as mybir
+from concourse.masks import make_identity
+
+D, T, I, Q, E, J, U = 512, 2048, 512, 128, 512, 256, 1024
+FLOPS = 2 * D * I * (Q + J) + 2 * I * Q * E
+
+F32 = mybir.dt.float32
+BF16 = mybir.dt.bfloat16
+I32 = mybir.dt.int32
+U32 = mybir.dt.uint32
+U16 = mybir.dt.uint16
+U8 = mybir.dt.uint8
+FP8X4 = mybir.dt.float8_e4m3fn_x4
+ALU = mybir.AluOpType
+ACT = mybir.ActivationFunctionType
+AXIS_X = mybir.AxisListType.X
+
+P = 128
+PACK = 4
+BANK = 512
+
+
+def tile_attend_novel_soft_read_kernel(tc, query, keys_words, keys_scales, kept, kw1, lam, os_row, vals, offs, offs2, out):
+    nc = tc.nc
+    with ExitStack() as ctx:
+        sb = ctx.enter_context(tc.tile_pool(name="sb", bufs=1))
+        ps = ctx.enter_context(tc.psum_pool(name="ps", bufs=1))
+
+        def bank(tag, name):
+            return ps.tile([P, BANK], F32, tag=tag, name=name)
+
+        kept_list = sb.tile([P, J // 16], U16)
+        slot_list = sb.tile([P, I // 16], U16)
+        scale_pool = sb.tile([P, T], U8)
+        nc.gpsimd.memset(scale_pool[:].bitcast(I32), 0)
+        nc.sync.dma_start(kept_list[:], offs2)
+        kept_rows = kept.rearrange("(p t) u -> p t u", t=PACK)
+        kept_pool = [sb.tile([P, U], F32, name=f"kept_pool{t}") for t in range(PACK)]
+        for t in range(PACK):
+            nc.sync.dma_start(kept_pool[t][:], kept_rows[:, t, :])
+        for g in range(4):
+            nc.gpsimd.dma_start(scale_pool[32 * g : 32 * g + 4, :].bitcast(I32), keys_scales[0, 4 * g : 4 * g + 4, :].bitcast(I32))
+        nc.sync.dma_start(slot_list[:], offs)
+        query_raw = sb.tile([P, PACK, Q], F32)
+        nc.sync.dma_start(query_raw[:], query.rearrange("(p t) q -> p t q", t=PACK))
+        word_pool = sb.tile([P, T], I32)
+        nc.sync.dma_start(word_pool[:], keys_words[0].rearrange("p c r -> p (c r)").bitcast(I32))
+        kw_cols = sb.tile([P, J // P], F32)
+        lam_col = sb.tile([P, 1], F32)
+        os_cols = sb.tile([P, PACK], F32)
+        with nc.allow_non_contiguous_dma(reason="one value to a partition"):
+            nc.sync.dma_start(kw_cols[:], kw1.rearrange("o (c p) -> p (o c)", p=P))
+            nc.sync.dma_start(lam_col[:], lam.rearrange("o p -> p o"))
+            nc.sync.dma_start(os_cols[:], os_row.rearrange("o (p t) -> p (o t)", t=PACK))
+        val_pool = [sb.tile([P, T], F32, name=f"val_pool{b}") for b in range(E // P)]
+        for b in range(E // P):
+            nc.sync.dma_start(val_pool[b][:], vals[b * P : (b + 1) * P, :])
+
+        warm = sb.tile([P, 1], F32)
+        warm_out = sb.tile([P, 1], F32)
+        nc.vector.memset(warm[:], 0.0)
+        nc.scalar.activation(warm_out[:], warm[:], ACT.Exp)
+
+        ident = sb.tile([P, P], F32)
+        make_identity(nc, ident[:])
+
+        kept_g = sb.tile([P, PACK, J], F32)
+        for t in range(PACK):
+            nc.vector.tensor_copy(kept_g[:, t, :], kept_pool[t][:].indirect(kept_list[:]))
+        key_scales = sb.tile([P, I], U8, align_bytes=64)
+        nc.vector.tensor_copy(key_scales[:], scale_pool[:].indirect(slot_list[:]))
+        kept_bf = sb.tile([P, J, PACK], BF16, align_bytes=64)
+        nc.scalar.copy(kept_bf[:], kept_g[:].rearrange("p t j -> p j t"))
+        query_bf = sb.tile([P, Q, PACK], BF16, align_bytes=64)
+        nc.scalar.copy(query_bf[:], query_raw[:].rearrange("p t q -> p q t"))
+        kept_codes = sb.tile([P, J], U32, align_bytes=64)
+        kept_scales = sb.tile([P, J], U8, align_bytes=64)
+        nc.vector.quantize_mx(out=kept_codes[:].bitcast(FP8X4), scales=kept_scales[:], in_=kept_bf[:].rearrange("p j t -> p (j t)"))
+        query_codes = sb.tile([P, Q], U32, align_bytes=64)
+        query_scales = sb.tile([P, Q], U8, align_bytes=64)
+        nc.vector.quantize_mx(out=query_codes[:].bitcast(FP8X4), scales=query_scales[:], in_=query_bf[:].rearrange("p q t -> p (q t)"))
+        key_codes = sb.tile([P, I], U32, align_bytes=64)
+        nc.vector.tensor_copy(key_codes[:], word_pool[:].bitcast(U32).indirect(slot_list[:]))
+
+        os_bank = bank("os", "os_bank")
+        for t in range(PACK):
+            nc.tensor.transpose(os_bank[:, t * P : (t + 1) * P], os_cols[:, t : t + 1].to_broadcast([P, P]), ident[:])
+
+        val_codes = sb.tile([P, E], U32, align_bytes=64)
+        val_scales = sb.tile([P, E], U8, align_bytes=64)
+
+        def turn_words(src_bf, turned, dst_bf):
+            words = src_bf[:].bitcast(F32)
+            for u in range(2):
+                nc.tensor.transpose(turned[:, u * P : (u + 1) * P], words[:, u : 2 * P : 2], ident[:])
+            nc.scalar.copy(
+                dst_bf[:].bitcast(F32).rearrange("p (r u) -> p r u", u=2),
+                turned[:, : 2 * P].rearrange("p (u r) -> p r u", u=2),
+            )
+
+        def gather_vals(b):
+            picked = sb.tile([P, I], BF16, name=f"val_picked{b}")
+            nc.vector.tensor_copy(picked[:], val_pool[b][:].indirect(slot_list[:]))
+            turned = bank(f"val{b % 2}", f"val_turned{b}")
+            val_bf = sb.tile([P, P * PACK], BF16, name=f"val_bf{b}", align_bytes=64)
+            turn_words(picked, turned, val_bf)
+            return val_bf
+
+        def quantise_vals(b, val_bf):
+            cols = slice(b * P, (b + 1) * P)
+            nc.vector.quantize_mx(out=val_codes[:, cols].bitcast(FP8X4), scales=val_scales[:, cols], in_=val_bf[:])
+
+        kk = [bank(f"kk{c}", f"kk{c}") for c in range(J // P)]
+        for c in range(J // P):
+            cols = slice(c * P, (c + 1) * P)
+            nc.tensor.matmul_mx(out=kk[c][:], lhsT=kept_codes[:, cols].bitcast(FP8X4), lhsT_scale=kept_scales[:, cols],
+                                rhs=key_codes[:].bitcast(FP8X4), rhs_scale=key_scales[:], start=True, stop=True)
+        a0 = bank("a0", "a0")
+        nc.tensor.matmul_mx(out=a0[:], lhsT=query_codes[:].bitcast(FP8X4), lhsT_scale=query_scales[:],
+                            rhs=key_codes[:].bitcast(FP8X4), rhs_scale=key_scales[:], start=True, stop=True)
+        weighted0 = sb.tile([P, I], F32)
+        nc.scalar.activation(weighted0[:], kk[0][:], ACT.Copy, scale=kw_cols[:, 0:1])
+        pair_max = sb.tile([P, I], F32)
+        nc.vector.scalar_tensor_tensor(pair_max[:], kk[1][:], kw_cols[:, 1:2], weighted0[:], ALU.mult, ALU.max)
+        a0_sb = sb.tile([P, I], F32)
+        nc.scalar.copy(a0_sb[:], a0[:])
+        val_bf0 = gather_vals(0)
+
+        max_turned = bank("turn", "max_turned")
+        for r in range(I // P):
+            nc.tensor.transpose(max_turned[:, r * P : (r + 1) * P], pair_max[:, r * P : (r + 1) * P], ident[:])
+        neg_m1 = sb.tile([P, I // P], F32)
+        nc.vector.tensor_reduce(neg_m1[:], max_turned[:].rearrange("p (r j) -> p r j", j=P), AXIS_X, ALU.max, negate=True)
+        quantise_vals(0, val_bf0)
+        m1_rows = bank("kk0", "m1_rows")
+        for r in range(I // P):
+            nc.tensor.transpose(m1_rows[:, r * P : (r + 1) * P], neg_m1[:, r : r + 1].to_broadcast([P, P]), ident[:])
+        scores = sb.tile([P, I], F32)
+        nc.vector.scalar_tensor_tensor(scores[:], m1_rows[:], lam_col[:], a0_sb[:], ALU.mult, ALU.add)
+        neg_max = sb.tile([P, 1], F32)
+        nc.vector.tensor_reduce(neg_max[:], scores[:], AXIS_X, ALU.max, negate=True)
+        val_bf1 = gather_vals(1)
+        probs = sb.tile([P, I], F32)
+        row_sum = sb.tile([P, 1], F32)
+        nc.scalar.activation(probs[:], scores[:], ACT.Exp, bias=neg_max[:], accum_out=row_sum[:])
+        inv_sum = sb.tile([P, 1], F32)
+        nc.vector.reciprocal(inv_sum[:], row_sum[:])
+        quantise_vals(1, val_bf1)
+        weights = sb.tile([P, I], BF16)
+        nc.vector.scalar_tensor_tensor(
+            weights[:].rearrange("p (n t) -> p n t", t=PACK), probs[:].rearrange("p (n t) -> p n t", t=PACK), inv_sum[:],
+            os_bank[:].rearrange("p (t n) -> p n t", t=PACK), ALU.mult, ALU.mult)
+        val_bf2 = gather_vals(2)
+        weight_bf = sb.tile([P, Q * PACK], BF16, align_bytes=64)
+        turn_words(weights, bank("kk1", "weights_turned"), weight_bf)
+        weight_codes = sb.tile([P, Q], U32, align_bytes=64)
+        weight_scales = sb.tile([P, Q], U8, align_bytes=64)
+        nc.vector.quantize_mx(out=weight_codes[:].bitcast(FP8X4), scales=weight_scales[:], in_=weight_bf[:])
+        quantise_vals(2, val_bf2)
+        val_bf3 = gather_vals(3)
+
+        def product(dst, cols):
+            nc.tensor.matmul_mx(out=dst, lhsT=weight_codes[:].bitcast(FP8X4), lhsT_scale=weight_scales[:],
+                                rhs=val_codes[:, cols].bitcast(FP8X4), rhs_scale=val_scales[:, cols], start=True, stop=True)
+
+        early = bank("a0", "out_early")
+        product(early[:, 0:256], slice(0, 256))
+        product(early[:, 256:384], slice(256, 384))
+        early_sb = sb.tile([P, 384], F32)
+        nc.scalar.copy(early_sb[:], early[:, 0:384])
+        nc.sync.dma_start(out[:, 0:384], early_sb[:])
+
+        quantise_vals(3, val_bf3)
+        late = bank("late", "out_late")
+        product(late[:, 0:128], slice(384, 512))
+        late_sb = sb.tile([P, 128], F32)
+        nc.vector.tensor_copy(late_sb[:], late[:, 0:128])
+        nc.sync.dma_start(out[:, 384:512], late_sb[:])

@@ -20,6 +20,8 @@ AXIS_X = mybir.AxisListType.X
 P = 128
 PACK = 4
 BANK = 512
+HALF = I // 2
+LAM_ROW = J // P
 
 
 def tile_attend_novel_soft_read_kernel(tc, query, keys_words, keys_scales, kept, kw1, lam, os_row, vals, offs, offs2, out):
@@ -35,26 +37,26 @@ def tile_attend_novel_soft_read_kernel(tc, query, keys_words, keys_scales, kept,
         slot_list = sb.tile([P, I // 16], U16)
         scale_pool = sb.tile([P, T], U8)
         nc.gpsimd.memset(scale_pool[:].bitcast(I32), 0)
+        kw_rows = sb.tile([P, P], F32)
+        nc.gpsimd.memset(kw_rows[:], 0.0)
+        rows = sb.tile([P, P], F32)
+        nc.gpsimd.memset(rows[:], 0.0)
         nc.sync.dma_start(kept_list[:], offs2)
-        kept_rows = kept.rearrange("(p t) u -> p t u", t=PACK)
-        kept_pool = [sb.tile([P, U], F32, name=f"kept_pool{t}") for t in range(PACK)]
-        for t in range(PACK):
-            nc.sync.dma_start(kept_pool[t][:], kept_rows[:, t, :])
-        for g in range(4):
-            nc.gpsimd.dma_start(scale_pool[32 * g : 32 * g + 4, :].bitcast(I32), keys_scales[0, 4 * g : 4 * g + 4, :].bitcast(I32))
         nc.sync.dma_start(slot_list[:], offs)
-        query_raw = sb.tile([P, PACK, Q], F32)
-        nc.sync.dma_start(query_raw[:], query.rearrange("(p t) q -> p t q", t=PACK))
+        kept_rows = kept.rearrange("(p t) u -> p t u", t=PACK)
+        kept_pool = [sb.tile([P, 2, U], F32, name=f"kept_pool{h}") for h in range(2)]
+        nc.sync.dma_start(kept_pool[0][:], kept_rows[:, 0:2, :])
+        for g in range(4):
+            nc.sync.dma_start(scale_pool[32 * g : 32 * g + 4, :].bitcast(I32), keys_scales[0, 4 * g : 4 * g + 4, :].bitcast(I32))
+        nc.sync.dma_start(kept_pool[1][:], kept_rows[:, 2:4, :])
+        nc.sync.dma_start(kw_rows[0 : J // P, :], kw1.rearrange("o (c n) -> (o c) n", n=P))
+        nc.sync.dma_start(kw_rows[LAM_ROW : LAM_ROW + 1, :], lam)
         word_pool = sb.tile([P, T], I32)
         nc.sync.dma_start(word_pool[:], keys_words[0].rearrange("p c r -> p (c r)").bitcast(I32))
-        kw_cols = sb.tile([P, J // P], F32)
-        lam_col = sb.tile([P, 1], F32)
-        os_cols = sb.tile([P, PACK], F32)
-        with nc.allow_non_contiguous_dma(reason="one value to a partition"):
-            nc.sync.dma_start(kw_cols[:], kw1.rearrange("o (c p) -> p (o c)", p=P))
-            nc.sync.dma_start(lam_col[:], lam.rearrange("o p -> p o"))
-            nc.sync.dma_start(os_cols[:], os_row.rearrange("o (p t) -> p (o t)", t=PACK))
-        val_pool = [sb.tile([P, T], F32, name=f"val_pool{b}") for b in range(E // P)]
+        query_raw = sb.tile([P, PACK, Q], F32)
+        nc.sync.dma_start(query_raw[:], query.rearrange("(p t) q -> p t q", t=PACK))
+        nc.sync.dma_start(rows[0 : I // P, :], os_row.rearrange("o (c n) -> (o c) n", n=P))
+        val_pool = [sb.tile([P, T], F32, tag=f"val{b}", name=f"val_pool{b}", align_bytes=64) for b in range(E // P)]
         for b in range(E // P):
             nc.sync.dma_start(val_pool[b][:], vals[b * P : (b + 1) * P, :])
 
@@ -66,115 +68,143 @@ def tile_attend_novel_soft_read_kernel(tc, query, keys_words, keys_scales, kept,
         ident = sb.tile([P, P], F32)
         make_identity(nc, ident[:])
 
-        kept_g = sb.tile([P, PACK, J], F32)
-        for t in range(PACK):
-            nc.vector.tensor_copy(kept_g[:, t, :], kept_pool[t][:].indirect(kept_list[:]))
+        kept_bf = sb.tile([P, J, PACK], BF16, align_bytes=64)
+        kept_picked = sb.tile([P, 2, J], F32)
+        for t in range(2):
+            nc.vector.tensor_copy(kept_picked[:, t, :], kept_pool[0][:, t, :].indirect(kept_list[:]))
+        nc.scalar.copy(kept_bf[:, :, 0:2], kept_picked[:].rearrange("p t j -> p j t"))
         key_scales = sb.tile([P, I], U8, align_bytes=64)
         nc.vector.tensor_copy(key_scales[:], scale_pool[:].indirect(slot_list[:]))
-        kept_bf = sb.tile([P, J, PACK], BF16, align_bytes=64)
-        nc.scalar.copy(kept_bf[:], kept_g[:].rearrange("p t j -> p j t"))
-        query_bf = sb.tile([P, Q, PACK], BF16, align_bytes=64)
-        nc.scalar.copy(query_bf[:], query_raw[:].rearrange("p t q -> p q t"))
+        for t in range(2):
+            nc.vector.tensor_copy(kept_bf[:, :, 2 + t], kept_pool[1][:, t, :].indirect(kept_list[:]))
         kept_codes = sb.tile([P, J], U32, align_bytes=64)
         kept_scales = sb.tile([P, J], U8, align_bytes=64)
         nc.vector.quantize_mx(out=kept_codes[:].bitcast(FP8X4), scales=kept_scales[:], in_=kept_bf[:].rearrange("p j t -> p (j t)"))
+        key_codes = sb.tile([P, I], U32, align_bytes=64)
+        for h in range(2):
+            nc.vector.tensor_copy(key_codes[:, h * HALF : (h + 1) * HALF],
+                                  word_pool[:].bitcast(U32).indirect(slot_list[:, h * HALF // 16 : (h + 1) * HALF // 16]))
+
+        query_bf = sb.tile([P, Q, PACK], BF16, align_bytes=64)
+        nc.scalar.copy(query_bf[:], query_raw[:].rearrange("p t q -> p q t"))
         query_codes = sb.tile([P, Q], U32, align_bytes=64)
         query_scales = sb.tile([P, Q], U8, align_bytes=64)
         nc.vector.quantize_mx(out=query_codes[:].bitcast(FP8X4), scales=query_scales[:], in_=query_bf[:].rearrange("p q t -> p (q t)"))
-        key_codes = sb.tile([P, I], U32, align_bytes=64)
-        nc.vector.tensor_copy(key_codes[:], word_pool[:].bitcast(U32).indirect(slot_list[:]))
+        kw_turned = bank("val0", "kw_turned")
+        nc.tensor.transpose(kw_turned[:, 0:P], kw_rows[:], ident[:])
+        kw_cols = sb.tile([P, LAM_ROW + 1], F32)
+        nc.scalar.copy(kw_cols[:], kw_turned[:, 0 : LAM_ROW + 1])
+        lam_bank = bank("late", "lam_bank")
+        nc.tensor.transpose(lam_bank[:, 0:P], kw_cols[:, LAM_ROW : LAM_ROW + 1].to_broadcast([P, P]), ident[:])
+        lam_rows = sb.tile([P, Q], F32)
+        nc.scalar.copy(lam_rows[:], lam_bank[:, 0:P])
 
-        os_bank = bank("os", "os_bank")
-        for t in range(PACK):
-            nc.tensor.transpose(os_bank[:, t * P : (t + 1) * P], os_cols[:, t : t + 1].to_broadcast([P, P]), ident[:])
+        val_bf = sb.tile([P, E * PACK], BF16, align_bytes=64)
+        picked = [sb.tile([P, I], BF16, name=f"val_picked{b}") for b in range(E // P)]
 
-        val_codes = sb.tile([P, E], U32, align_bytes=64)
-        val_scales = sb.tile([P, E], U8, align_bytes=64)
-
-        def turn_words(src_bf, turned, dst_bf):
-            words = src_bf[:].bitcast(F32)
-            for u in range(2):
-                nc.tensor.transpose(turned[:, u * P : (u + 1) * P], words[:, u : 2 * P : 2], ident[:])
+        def turn_words(sources, turned, dst_bf):
+            n = len(sources)
+            for b, src_bf in enumerate(sources):
+                words = src_bf.bitcast(F32)
+                for u in range(2):
+                    at = (2 * b + u) * P
+                    nc.tensor.transpose(turned[:, at : at + P], words[:, u : 2 * P : 2], ident[:])
             nc.scalar.copy(
-                dst_bf[:].bitcast(F32).rearrange("p (r u) -> p r u", u=2),
-                turned[:, : 2 * P].rearrange("p (u r) -> p r u", u=2),
+                dst_bf.bitcast(F32).rearrange("p (b r u) -> p b r u", b=n, u=2),
+                turned[:, : 2 * n * P].rearrange("p (b u r) -> p b r u", b=n, u=2),
             )
 
         def gather_vals(b):
-            picked = sb.tile([P, I], BF16, name=f"val_picked{b}")
-            nc.vector.tensor_copy(picked[:], val_pool[b][:].indirect(slot_list[:]))
-            turned = bank(f"val{b % 2}", f"val_turned{b}")
-            val_bf = sb.tile([P, P * PACK], BF16, name=f"val_bf{b}", align_bytes=64)
-            turn_words(picked, turned, val_bf)
-            return val_bf
+            nc.vector.tensor_copy(picked[b][:], val_pool[b][:].indirect(slot_list[:]))
 
-        def quantise_vals(b, val_bf):
-            cols = slice(b * P, (b + 1) * P)
-            nc.vector.quantize_mx(out=val_codes[:, cols].bitcast(FP8X4), scales=val_scales[:, cols], in_=val_bf[:])
+        def turn_vals(lo, hi, tag):
+            turn_words([picked[b][:] for b in range(lo, hi)], bank(tag, f"val_turned{lo}"), val_bf[:, lo * P * PACK : hi * P * PACK])
 
-        kk = [bank(f"kk{c}", f"kk{c}") for c in range(J // P)]
-        for c in range(J // P):
-            cols = slice(c * P, (c + 1) * P)
-            nc.tensor.matmul_mx(out=kk[c][:], lhsT=kept_codes[:, cols].bitcast(FP8X4), lhsT_scale=kept_scales[:, cols],
-                                rhs=key_codes[:].bitcast(FP8X4), rhs_scale=key_scales[:], start=True, stop=True)
-        a0 = bank("a0", "a0")
-        nc.tensor.matmul_mx(out=a0[:], lhsT=query_codes[:].bitcast(FP8X4), lhsT_scale=query_scales[:],
-                            rhs=key_codes[:].bitcast(FP8X4), rhs_scale=key_scales[:], start=True, stop=True)
         weighted0 = sb.tile([P, I], F32)
-        nc.scalar.activation(weighted0[:], kk[0][:], ACT.Copy, scale=kw_cols[:, 0:1])
         pair_max = sb.tile([P, I], F32)
-        nc.vector.scalar_tensor_tensor(pair_max[:], kk[1][:], kw_cols[:, 1:2], weighted0[:], ALU.mult, ALU.max)
-        a0_sb = sb.tile([P, I], F32)
+        for h in range(2):
+            slots = slice(h * HALF, (h + 1) * HALF)
+            kk = [bank(tag, f"kk{h}{c}") for c, tag in enumerate((("kk0", "kk1"), ("val0", "val1"))[h])]
+            for c in range(J // P):
+                cols = slice(c * P, (c + 1) * P)
+                nc.tensor.matmul_mx(out=kk[c][:, :HALF], lhsT=kept_codes[:, cols].bitcast(FP8X4), lhsT_scale=kept_scales[:, cols],
+                                    rhs=key_codes[:, slots].bitcast(FP8X4), rhs_scale=key_scales[:, slots], start=True, stop=True)
+            nc.scalar.activation(weighted0[:, slots], kk[0][:, :HALF], ACT.Copy, scale=kw_cols[:, 0:1])
+            nc.vector.scalar_tensor_tensor(pair_max[:, slots], kk[1][:, :HALF], kw_cols[:, 1:2], weighted0[:, slots], ALU.mult, ALU.max)
+        a0 = bank("a0", "a0")
+        for r in range(I // P):
+            cols = slice(r * P, (r + 1) * P)
+            nc.tensor.matmul_mx(out=a0[:, cols], lhsT=key_codes[:, cols].bitcast(FP8X4), lhsT_scale=key_scales[:, cols],
+                                rhs=query_codes[:].bitcast(FP8X4), rhs_scale=query_scales[:], start=True, stop=True)
+        a0_sb = sb.tile([P, I // P * Q], F32)
         nc.scalar.copy(a0_sb[:], a0[:])
-        val_bf0 = gather_vals(0)
 
-        max_turned = bank("turn", "max_turned")
+
+        gather_vals(0)
+        neg_m1 = sb.tile([P, I // P], F32, tag="val0", align_bytes=64)
+        for h, tag in enumerate(("turn", "kk1")):
+            turned = bank(tag, f"max_turned{h}")
+            for r in range(2):
+                at = h * HALF + r * P
+                nc.tensor.transpose(turned[:, r * P : (r + 1) * P], pair_max[:, at : at + P], ident[:])
+            nc.vector.tensor_reduce(neg_m1[:, 2 * h : 2 * h + 2], turned[:, :HALF].rearrange("p (r j) -> p r j", j=P), AXIS_X, ALU.max, negate=True)
+        scores = bank("kk0", "scores")
         for r in range(I // P):
-            nc.tensor.transpose(max_turned[:, r * P : (r + 1) * P], pair_max[:, r * P : (r + 1) * P], ident[:])
-        neg_m1 = sb.tile([P, I // P], F32)
-        nc.vector.tensor_reduce(neg_m1[:], max_turned[:].rearrange("p (r j) -> p r j", j=P), AXIS_X, ALU.max, negate=True)
-        quantise_vals(0, val_bf0)
-        m1_rows = bank("kk0", "m1_rows")
+            cols = slice(r * P, (r + 1) * P)
+            nc.tensor.matmul(scores[:, cols], a0_sb[:, cols], ident[:], start=(r == 0), stop=False, is_transpose=True)
+        penalty = sb.tile([P, I // P * Q], F32)
         for r in range(I // P):
-            nc.tensor.transpose(m1_rows[:, r * P : (r + 1) * P], neg_m1[:, r : r + 1].to_broadcast([P, P]), ident[:])
-        scores = sb.tile([P, I], F32)
-        nc.vector.scalar_tensor_tensor(scores[:], m1_rows[:], lam_col[:], a0_sb[:], ALU.mult, ALU.add)
-        neg_max = sb.tile([P, 1], F32)
+            cols = slice(r * P, (r + 1) * P)
+            nc.scalar.activation(penalty[:, cols], lam_rows[:], ACT.Copy, scale=neg_m1[:, r : r + 1])
+            nc.tensor.matmul(scores[:, cols], penalty[:, cols], ident[:], start=False, stop=(r == I // P - 1), is_transpose=True)
+        rows_turned = bank("late", "rows_turned")
+        nc.tensor.transpose(rows_turned[:, 0:P], rows[:], ident[:])
+        columns = sb.tile([P, I // P], F32, tag="val0", align_bytes=64)
+        nc.scalar.copy(columns[:], rows_turned[:, 0 : I // P])
+        os_bank = bank("os", "os_bank")
+        for c in range(I // P):
+            nc.tensor.transpose(os_bank[:, c * P : (c + 1) * P], columns[:, c : c + 1].to_broadcast([P, P]), ident[:])
+        gather_vals(1)
+        neg_max = sb.tile([P, 1], F32, tag="val1", align_bytes=64)
         nc.vector.tensor_reduce(neg_max[:], scores[:], AXIS_X, ALU.max, negate=True)
-        val_bf1 = gather_vals(1)
         probs = sb.tile([P, I], F32)
         row_sum = sb.tile([P, 1], F32)
         nc.scalar.activation(probs[:], scores[:], ACT.Exp, bias=neg_max[:], accum_out=row_sum[:])
-        inv_sum = sb.tile([P, 1], F32)
+        gather_vals(2)
+        turn_vals(0, 2, "kk0")
+        inv_sum = sb.tile([P, 1], F32, tag="val2", align_bytes=64)
         nc.vector.reciprocal(inv_sum[:], row_sum[:])
-        quantise_vals(1, val_bf1)
         weights = sb.tile([P, I], BF16)
-        nc.vector.scalar_tensor_tensor(
-            weights[:].rearrange("p (n t) -> p n t", t=PACK), probs[:].rearrange("p (n t) -> p n t", t=PACK), inv_sum[:],
-            os_bank[:].rearrange("p (t n) -> p n t", t=PACK), ALU.mult, ALU.mult)
-        val_bf2 = gather_vals(2)
+        nc.vector.scalar_tensor_tensor(weights[:], probs[:], inv_sum[:], os_bank[:], ALU.mult, ALU.mult)
+        turn_vals(2, 3, "val0")
+        gather_vals(3)
         weight_bf = sb.tile([P, Q * PACK], BF16, align_bytes=64)
-        turn_words(weights, bank("kk1", "weights_turned"), weight_bf)
-        weight_codes = sb.tile([P, Q], U32, align_bytes=64)
-        weight_scales = sb.tile([P, Q], U8, align_bytes=64)
-        nc.vector.quantize_mx(out=weight_codes[:].bitcast(FP8X4), scales=weight_scales[:], in_=weight_bf[:])
-        quantise_vals(2, val_bf2)
-        val_bf3 = gather_vals(3)
+        turn_words([weights[:]], bank("kk1", "weights_turned"), weight_bf[:])
+        turn_vals(3, 4, "val1")
+        codes = sb.tile([P, Q + E], U32, tag="val3", align_bytes=64)
+        scales = sb.tile([P, Q + E], U8, align_bytes=64)
 
-        def product(dst, cols):
-            nc.tensor.matmul_mx(out=dst, lhsT=weight_codes[:].bitcast(FP8X4), lhsT_scale=weight_scales[:],
-                                rhs=val_codes[:, cols].bitcast(FP8X4), rhs_scale=val_scales[:, cols], start=True, stop=True)
+        def quantise_vals(lo, hi):
+            nc.vector.quantize_mx(out=codes[:, Q + lo : Q + hi].bitcast(FP8X4), scales=scales[:, Q + lo : Q + hi],
+                                  in_=val_bf[:, lo * PACK : hi * PACK])
 
+        def product(dst, lo, hi):
+            nc.tensor.matmul_mx(out=dst, lhsT=codes[:, :Q].bitcast(FP8X4), lhsT_scale=scales[:, :Q],
+                                rhs=codes[:, Q + lo : Q + hi].bitcast(FP8X4), rhs_scale=scales[:, Q + lo : Q + hi], start=True, stop=True)
+
+        quantise_vals(0, 256)
+        nc.vector.quantize_mx(out=codes[:, :Q].bitcast(FP8X4), scales=scales[:, :Q], in_=weight_bf[:])
+        quantise_vals(256, 384)
         early = bank("a0", "out_early")
-        product(early[:, 0:256], slice(0, 256))
-        product(early[:, 256:384], slice(256, 384))
+        product(early[:, 0:256], 0, 256)
+        product(early[:, 256:384], 256, 384)
         early_sb = sb.tile([P, 384], F32)
         nc.scalar.copy(early_sb[:], early[:, 0:384])
         nc.sync.dma_start(out[:, 0:384], early_sb[:])
 
-        quantise_vals(3, val_bf3)
+        quantise_vals(384, 512)
         late = bank("late", "out_late")
-        product(late[:, 0:128], slice(384, 512))
+        product(late[:, 0:128], 384, 512)
         late_sb = sb.tile([P, 128], F32)
         nc.vector.tensor_copy(late_sb[:], late[:, 0:128])
         nc.sync.dma_start(out[:, 384:512], late_sb[:])

@@ -20,8 +20,11 @@ AXIS_X = mybir.AxisListType.X
 P = 128
 PACK = 4
 BANK = 512
+LIST_ROWS = 16
+QUADRANT = 32
 HALF = I // 2
 LAM_ROW = J // P
+EARLY = E - P
 
 
 def tile_attend_novel_soft_read_kernel(tc, query, keys_words, keys_scales, kept, kw1, lam, os_row, vals, offs, offs2, out):
@@ -33,37 +36,34 @@ def tile_attend_novel_soft_read_kernel(tc, query, keys_words, keys_scales, kept,
         def bank(tag, name):
             return ps.tile([P, BANK], F32, tag=tag, name=name)
 
-        kept_list = sb.tile([P, J // 16], U16)
-        slot_list = sb.tile([P, I // 16], U16)
+        kept_list = sb.tile([P, J // LIST_ROWS], U16)
+        slot_list = sb.tile([P, I // LIST_ROWS], U16)
         scale_pool = sb.tile([P, T], U8)
         nc.gpsimd.memset(scale_pool[:].bitcast(I32), 0)
         kw_rows = sb.tile([P, P], F32)
         nc.gpsimd.memset(kw_rows[:], 0.0)
-        rows = sb.tile([P, P], F32)
-        nc.gpsimd.memset(rows[:], 0.0)
+        os_rows = sb.tile([P, P], F32)
+        nc.gpsimd.memset(os_rows[:], 0.0)
+        kept_planes = kept.rearrange("(p t) u -> p t u", t=PACK)
+        kept_pool = [sb.tile([P, 2, U], F32, name=f"kept_pool{h}") for h in range(2)]
+        nc.sync.dma_start(kept_pool[0][:], kept_planes[:, 0:2, :])
         nc.sync.dma_start(kept_list[:], offs2)
         nc.sync.dma_start(slot_list[:], offs)
-        kept_rows = kept.rearrange("(p t) u -> p t u", t=PACK)
-        kept_pool = [sb.tile([P, 2, U], F32, name=f"kept_pool{h}") for h in range(2)]
-        nc.sync.dma_start(kept_pool[0][:], kept_rows[:, 0:2, :])
-        for g in range(4):
-            nc.sync.dma_start(scale_pool[32 * g : 32 * g + 4, :].bitcast(I32), keys_scales[0, 4 * g : 4 * g + 4, :].bitcast(I32))
-        nc.sync.dma_start(kept_pool[1][:], kept_rows[:, 2:4, :])
+        for g in range(P // QUADRANT):
+            nc.sync.dma_start(
+                scale_pool[QUADRANT * g : QUADRANT * g + 4, :].bitcast(I32), keys_scales[0, 4 * g : 4 * g + 4, :].bitcast(I32)
+            )
+        nc.sync.dma_start(kept_pool[1][:], kept_planes[:, 2:4, :])
         nc.sync.dma_start(kw_rows[0 : J // P, :], kw1.rearrange("o (c n) -> (o c) n", n=P))
         nc.sync.dma_start(kw_rows[LAM_ROW : LAM_ROW + 1, :], lam)
         word_pool = sb.tile([P, T], I32)
         nc.sync.dma_start(word_pool[:], keys_words[0].rearrange("p c r -> p (c r)").bitcast(I32))
         query_raw = sb.tile([P, PACK, Q], F32)
         nc.sync.dma_start(query_raw[:], query.rearrange("(p t) q -> p t q", t=PACK))
-        nc.sync.dma_start(rows[0 : I // P, :], os_row.rearrange("o (c n) -> (o c) n", n=P))
+        nc.sync.dma_start(os_rows[0 : I // P, :], os_row.rearrange("o (c n) -> (o c) n", n=P))
         val_pool = [sb.tile([P, T], F32, tag=f"val{b}", name=f"val_pool{b}", align_bytes=64) for b in range(E // P)]
         for b in range(E // P):
             nc.sync.dma_start(val_pool[b][:], vals[b * P : (b + 1) * P, :])
-
-        warm = sb.tile([P, 1], F32)
-        warm_out = sb.tile([P, 1], F32)
-        nc.vector.memset(warm[:], 0.0)
-        nc.scalar.activation(warm_out[:], warm[:], ACT.Exp)
 
         ident = sb.tile([P, P], F32)
         make_identity(nc, ident[:])
@@ -72,7 +72,7 @@ def tile_attend_novel_soft_read_kernel(tc, query, keys_words, keys_scales, kept,
         kept_picked = sb.tile([P, 2, J], F32)
         for t in range(2):
             nc.vector.tensor_copy(kept_picked[:, t, :], kept_pool[0][:, t, :].indirect(kept_list[:]))
-        nc.scalar.copy(kept_bf[:, :, 0:2], kept_picked[:].rearrange("p t j -> p j t"))
+        nc.scalar.activation(kept_bf[:, :, 0:2], kept_picked[:].rearrange("p t j -> p j t"), ACT.Copy)
         key_scales = sb.tile([P, I], U8, align_bytes=64)
         nc.vector.tensor_copy(key_scales[:], scale_pool[:].indirect(slot_list[:]))
         for t in range(2):
@@ -82,14 +82,15 @@ def tile_attend_novel_soft_read_kernel(tc, query, keys_words, keys_scales, kept,
         nc.vector.quantize_mx(out=kept_codes[:].bitcast(FP8X4), scales=kept_scales[:], in_=kept_bf[:].rearrange("p j t -> p (j t)"))
         key_codes = sb.tile([P, I], U32, align_bytes=64)
         for h in range(2):
-            nc.vector.tensor_copy(key_codes[:, h * HALF : (h + 1) * HALF],
-                                  word_pool[:].bitcast(U32).indirect(slot_list[:, h * HALF // 16 : (h + 1) * HALF // 16]))
+            entries = slot_list[:, h * HALF // LIST_ROWS : (h + 1) * HALF // LIST_ROWS]
+            nc.vector.tensor_copy(key_codes[:, h * HALF : (h + 1) * HALF], word_pool[:].bitcast(U32).indirect(entries))
 
         query_bf = sb.tile([P, Q, PACK], BF16, align_bytes=64)
         nc.scalar.copy(query_bf[:], query_raw[:].rearrange("p t q -> p q t"))
         query_codes = sb.tile([P, Q], U32, align_bytes=64)
         query_scales = sb.tile([P, Q], U8, align_bytes=64)
         nc.vector.quantize_mx(out=query_codes[:].bitcast(FP8X4), scales=query_scales[:], in_=query_bf[:].rearrange("p q t -> p (q t)"))
+
         kw_turned = bank("val0", "kw_turned")
         nc.tensor.transpose(kw_turned[:, 0:P], kw_rows[:], ident[:])
         kw_cols = sb.tile([P, LAM_ROW + 1], F32)
@@ -99,55 +100,64 @@ def tile_attend_novel_soft_read_kernel(tc, query, keys_words, keys_scales, kept,
         lam_rows = sb.tile([P, Q], F32)
         nc.scalar.copy(lam_rows[:], lam_bank[:, 0:P])
 
-        val_bf = sb.tile([P, E * PACK], BF16, align_bytes=64)
         picked = [sb.tile([P, I], BF16, name=f"val_picked{b}") for b in range(E // P)]
 
-        def turn_words(sources, turned, dst_bf):
-            n = len(sources)
-            for b, src_bf in enumerate(sources):
-                words = src_bf.bitcast(F32)
+        def turn(sources, turned):
+            for b, source in enumerate(sources):
+                words = source.bitcast(F32)
                 for u in range(2):
                     at = (2 * b + u) * P
                     nc.tensor.transpose(turned[:, at : at + P], words[:, u : 2 * P : 2], ident[:])
+
+        def weave(turned, count, dst_bf):
             nc.scalar.copy(
-                dst_bf.bitcast(F32).rearrange("p (b r u) -> p b r u", b=n, u=2),
-                turned[:, : 2 * n * P].rearrange("p (b u r) -> p b r u", b=n, u=2),
+                dst_bf.bitcast(F32).rearrange("p (b r u) -> p b r u", b=count, u=2),
+                turned[:, : 2 * count * P].rearrange("p (b u r) -> p b r u", b=count, u=2),
             )
 
         def gather_vals(b):
             nc.vector.tensor_copy(picked[b][:], val_pool[b][:].indirect(slot_list[:]))
 
         def turn_vals(lo, hi, tag):
-            turn_words([picked[b][:] for b in range(lo, hi)], bank(tag, f"val_turned{lo}"), val_bf[:, lo * P * PACK : hi * P * PACK])
+            turned = bank(tag, f"val_turned{lo}")
+            turn([picked[b][:] for b in range(lo, hi)], turned)
+            return turned
 
         weighted0 = sb.tile([P, I], F32)
         pair_max = sb.tile([P, I], F32)
-        for h in range(2):
+        for h, tags in enumerate((("kk0", "kk1"), ("val0", "val1"))):
             slots = slice(h * HALF, (h + 1) * HALF)
-            kk = [bank(tag, f"kk{h}{c}") for c, tag in enumerate((("kk0", "kk1"), ("val0", "val1"))[h])]
+            kk = [bank(tag, f"kk{h}{c}") for c, tag in enumerate(tags)]
             for c in range(J // P):
                 cols = slice(c * P, (c + 1) * P)
-                nc.tensor.matmul_mx(out=kk[c][:, :HALF], lhsT=kept_codes[:, cols].bitcast(FP8X4), lhsT_scale=kept_scales[:, cols],
-                                    rhs=key_codes[:, slots].bitcast(FP8X4), rhs_scale=key_scales[:, slots], start=True, stop=True)
+                nc.tensor.matmul_mx(
+                    out=kk[c][:, :HALF], lhsT=kept_codes[:, cols].bitcast(FP8X4), lhsT_scale=kept_scales[:, cols],
+                    rhs=key_codes[:, slots].bitcast(FP8X4), rhs_scale=key_scales[:, slots], start=True, stop=True,
+                )
             nc.scalar.activation(weighted0[:, slots], kk[0][:, :HALF], ACT.Copy, scale=kw_cols[:, 0:1])
             nc.vector.scalar_tensor_tensor(pair_max[:, slots], kk[1][:, :HALF], kw_cols[:, 1:2], weighted0[:, slots], ALU.mult, ALU.max)
+
         a0 = bank("a0", "a0")
         for r in range(I // P):
             cols = slice(r * P, (r + 1) * P)
-            nc.tensor.matmul_mx(out=a0[:, cols], lhsT=key_codes[:, cols].bitcast(FP8X4), lhsT_scale=key_scales[:, cols],
-                                rhs=query_codes[:].bitcast(FP8X4), rhs_scale=query_scales[:], start=True, stop=True)
+            nc.tensor.matmul_mx(
+                out=a0[:, cols], lhsT=key_codes[:, cols].bitcast(FP8X4), lhsT_scale=key_scales[:, cols],
+                rhs=query_codes[:].bitcast(FP8X4), rhs_scale=query_scales[:], start=True, stop=True,
+            )
         a0_sb = sb.tile([P, I // P * Q], F32)
         nc.scalar.copy(a0_sb[:], a0[:])
-
 
         gather_vals(0)
         neg_m1 = sb.tile([P, I // P], F32, tag="val0", align_bytes=64)
         for h, tag in enumerate(("turn", "kk1")):
-            turned = bank(tag, f"max_turned{h}")
+            max_turned = bank(tag, f"max_turned{h}")
             for r in range(2):
                 at = h * HALF + r * P
-                nc.tensor.transpose(turned[:, r * P : (r + 1) * P], pair_max[:, at : at + P], ident[:])
-            nc.vector.tensor_reduce(neg_m1[:, 2 * h : 2 * h + 2], turned[:, :HALF].rearrange("p (r j) -> p r j", j=P), AXIS_X, ALU.max, negate=True)
+                nc.tensor.transpose(max_turned[:, r * P : (r + 1) * P], pair_max[:, at : at + P], ident[:])
+            nc.vector.tensor_reduce(
+                neg_m1[:, 2 * h : 2 * h + 2], max_turned[:, :HALF].rearrange("p (r j) -> p r j", j=P), AXIS_X, ALU.max, negate=True
+            )
+
         scores = bank("kk0", "scores")
         for r in range(I // P):
             cols = slice(r * P, (r + 1) * P)
@@ -157,54 +167,64 @@ def tile_attend_novel_soft_read_kernel(tc, query, keys_words, keys_scales, kept,
             cols = slice(r * P, (r + 1) * P)
             nc.scalar.activation(penalty[:, cols], lam_rows[:], ACT.Copy, scale=neg_m1[:, r : r + 1])
             nc.tensor.matmul(scores[:, cols], penalty[:, cols], ident[:], start=False, stop=(r == I // P - 1), is_transpose=True)
-        rows_turned = bank("late", "rows_turned")
-        nc.tensor.transpose(rows_turned[:, 0:P], rows[:], ident[:])
-        columns = sb.tile([P, I // P], F32, tag="val0", align_bytes=64)
-        nc.scalar.copy(columns[:], rows_turned[:, 0 : I // P])
+
+        os_turned = bank("late", "os_turned")
+        nc.tensor.transpose(os_turned[:, 0:P], os_rows[:], ident[:])
+        os_cols = sb.tile([P, I // P], F32, tag="val0", align_bytes=64)
+        nc.scalar.copy(os_cols[:], os_turned[:, 0 : I // P])
         os_bank = bank("os", "os_bank")
         for c in range(I // P):
-            nc.tensor.transpose(os_bank[:, c * P : (c + 1) * P], columns[:, c : c + 1].to_broadcast([P, P]), ident[:])
+            nc.tensor.transpose(os_bank[:, c * P : (c + 1) * P], os_cols[:, c : c + 1].to_broadcast([P, P]), ident[:])
+
         gather_vals(1)
+        first_turned = turn_vals(0, 2, "late")
         neg_max = sb.tile([P, 1], F32, tag="val1", align_bytes=64)
         nc.vector.tensor_reduce(neg_max[:], scores[:], AXIS_X, ALU.max, negate=True)
         probs = sb.tile([P, I], F32)
         row_sum = sb.tile([P, 1], F32)
         nc.scalar.activation(probs[:], scores[:], ACT.Exp, bias=neg_max[:], accum_out=row_sum[:])
         gather_vals(2)
-        turn_vals(0, 2, "kk0")
+        val_bf = sb.tile([P, E * PACK], BF16, tag="val1", align_bytes=64)
+        weave(first_turned, 2, val_bf[:, 0 : 2 * P * PACK])
         inv_sum = sb.tile([P, 1], F32, tag="val2", align_bytes=64)
         nc.vector.reciprocal(inv_sum[:], row_sum[:])
         weights = sb.tile([P, I], BF16)
         nc.vector.scalar_tensor_tensor(weights[:], probs[:], inv_sum[:], os_bank[:], ALU.mult, ALU.mult)
-        turn_vals(2, 3, "val0")
+        weave(turn_vals(2, 3, "val0"), 1, val_bf[:, 2 * P * PACK : 3 * P * PACK])
         gather_vals(3)
         weight_bf = sb.tile([P, Q * PACK], BF16, align_bytes=64)
-        turn_words([weights[:]], bank("kk1", "weights_turned"), weight_bf[:])
-        turn_vals(3, 4, "val1")
+        weights_turned = bank("kk1", "weights_turned")
+        turn([weights[:]], weights_turned)
+        weave(weights_turned, 1, weight_bf[:])
+        weave(turn_vals(3, 4, "val1"), 1, val_bf[:, 3 * P * PACK :])
+
         codes = sb.tile([P, Q + E], U32, tag="val3", align_bytes=64)
         scales = sb.tile([P, Q + E], U8, align_bytes=64)
 
         def quantise_vals(lo, hi):
-            nc.vector.quantize_mx(out=codes[:, Q + lo : Q + hi].bitcast(FP8X4), scales=scales[:, Q + lo : Q + hi],
-                                  in_=val_bf[:, lo * PACK : hi * PACK])
+            nc.vector.quantize_mx(
+                out=codes[:, Q + lo : Q + hi].bitcast(FP8X4), scales=scales[:, Q + lo : Q + hi], in_=val_bf[:, lo * PACK : hi * PACK]
+            )
 
         def product(dst, lo, hi):
-            nc.tensor.matmul_mx(out=dst, lhsT=codes[:, :Q].bitcast(FP8X4), lhsT_scale=scales[:, :Q],
-                                rhs=codes[:, Q + lo : Q + hi].bitcast(FP8X4), rhs_scale=scales[:, Q + lo : Q + hi], start=True, stop=True)
+            nc.tensor.matmul_mx(
+                out=dst, lhsT=codes[:, :Q].bitcast(FP8X4), lhsT_scale=scales[:, :Q],
+                rhs=codes[:, Q + lo : Q + hi].bitcast(FP8X4), rhs_scale=scales[:, Q + lo : Q + hi], start=True, stop=True,
+            )
 
-        quantise_vals(0, 256)
+        quantise_vals(0, 2 * P)
         nc.vector.quantize_mx(out=codes[:, :Q].bitcast(FP8X4), scales=scales[:, :Q], in_=weight_bf[:])
-        quantise_vals(256, 384)
+        quantise_vals(2 * P, EARLY)
         early = bank("a0", "out_early")
-        product(early[:, 0:256], 0, 256)
-        product(early[:, 256:384], 256, 384)
-        early_sb = sb.tile([P, 384], F32)
-        nc.scalar.copy(early_sb[:], early[:, 0:384])
-        nc.sync.dma_start(out[:, 0:384], early_sb[:])
+        product(early[:, 0 : 2 * P], 0, 2 * P)
+        product(early[:, 2 * P : EARLY], 2 * P, EARLY)
+        early_sb = sb.tile([P, EARLY], F32)
+        nc.scalar.copy(early_sb[:], early[:, 0:EARLY])
+        nc.sync.dma_start(out[:, 0:EARLY], early_sb[:])
 
-        quantise_vals(384, 512)
+        quantise_vals(EARLY, E)
         late = bank("late", "out_late")
-        product(late[:, 0:128], 384, 512)
-        late_sb = sb.tile([P, 128], F32)
-        nc.vector.tensor_copy(late_sb[:], late[:, 0:128])
-        nc.sync.dma_start(out[:, 384:512], late_sb[:])
+        product(late[:, 0 : E - EARLY], EARLY, E)
+        late_sb = sb.tile([P, E - EARLY], F32)
+        nc.vector.tensor_copy(late_sb[:], late[:, 0 : E - EARLY])
+        nc.sync.dma_start(out[:, EARLY:E], late_sb[:])

from contextlib import ExitStack

import concourse.mybir as mybir
from concourse.masks import make_identity

D, T, I, Q, E, J, U = 512, 2048, 512, 128, 512, 256, 1024
FLOPS = 2 * D * I * (Q + J) + 2 * I * Q * E

F32 = mybir.dt.float32
BF16 = mybir.dt.bfloat16
I32 = mybir.dt.int32
U32 = mybir.dt.uint32
U16 = mybir.dt.uint16
U8 = mybir.dt.uint8
FP8X4 = mybir.dt.float8_e4m3fn_x4
ALU = mybir.AluOpType
ACT = mybir.ActivationFunctionType
AXIS_X = mybir.AxisListType.X

P = 128
PACK = 4
BANK = 512
LIST_ROWS = 16
QUADRANT = 32
HALF = I // 2
LAM_ROW = J // P
EARLY = E - P


def tile_attend_novel_soft_read_kernel(tc, query, keys_words, keys_scales, kept, kw1, lam, os_row, vals, offs, offs2, out):
    nc = tc.nc
    with ExitStack() as ctx:
        sb = ctx.enter_context(tc.tile_pool(name="sb", bufs=1))
        ps = ctx.enter_context(tc.psum_pool(name="ps", bufs=1))

        def bank(tag, name):
            return ps.tile([P, BANK], F32, tag=tag, name=name)

        kept_list = sb.tile([P, J // LIST_ROWS], U16)
        slot_list = sb.tile([P, I // LIST_ROWS], U16)
        scale_pool = sb.tile([P, T], U8)
        nc.gpsimd.memset(scale_pool[:].bitcast(I32), 0)
        kw_rows = sb.tile([P, P], F32)
        nc.gpsimd.memset(kw_rows[:], 0.0)
        os_rows = sb.tile([P, P], F32)
        nc.gpsimd.memset(os_rows[:], 0.0)
        kept_planes = kept.rearrange("(p t) u -> p t u", t=PACK)
        kept_pool = [sb.tile([P, 2, U], F32, name=f"kept_pool{h}") for h in range(2)]
        nc.sync.dma_start(kept_pool[0][:], kept_planes[:, 0:2, :])
        nc.sync.dma_start(kept_list[:], offs2)
        nc.sync.dma_start(slot_list[:], offs)
        for g in range(P // QUADRANT):
            nc.sync.dma_start(
                scale_pool[QUADRANT * g : QUADRANT * g + 4, :].bitcast(I32), keys_scales[0, 4 * g : 4 * g + 4, :].bitcast(I32)
            )
        nc.sync.dma_start(kept_pool[1][:], kept_planes[:, 2:4, :])
        nc.sync.dma_start(kw_rows[0 : J // P, :], kw1.rearrange("o (c n) -> (o c) n", n=P))
        nc.sync.dma_start(kw_rows[LAM_ROW : LAM_ROW + 1, :], lam)
        word_pool = sb.tile([P, T], I32)
        nc.sync.dma_start(word_pool[:], keys_words[0].rearrange("p c r -> p (c r)").bitcast(I32))
        query_raw = sb.tile([P, PACK, Q], F32)
        nc.sync.dma_start(query_raw[:], query.rearrange("(p t) q -> p t q", t=PACK))
        nc.sync.dma_start(os_rows[0 : I // P, :], os_row.rearrange("o (c n) -> (o c) n", n=P))
        val_pool = [sb.tile([P, T], F32, tag=f"val{b}", name=f"val_pool{b}", align_bytes=64) for b in range(E // P)]
        for b in range(E // P):
            nc.sync.dma_start(val_pool[b][:], vals[b * P : (b + 1) * P, :])

        ident = sb.tile([P, P], F32)
        make_identity(nc, ident[:])

        kept_bf = sb.tile([P, J, PACK], BF16, align_bytes=64)
        kept_picked = sb.tile([P, 2, J], F32)
        for t in range(2):
            nc.vector.tensor_copy(kept_picked[:, t, :], kept_pool[0][:, t, :].indirect(kept_list[:]))
        nc.scalar.activation(kept_bf[:, :, 0:2], kept_picked[:].rearrange("p t j -> p j t"), ACT.Copy)
        key_scales = sb.tile([P, I], U8, align_bytes=64)
        nc.vector.tensor_copy(key_scales[:], scale_pool[:].indirect(slot_list[:]))
        for t in range(2):
            nc.vector.tensor_copy(kept_bf[:, :, 2 + t], kept_pool[1][:, t, :].indirect(kept_list[:]))
        kept_codes = sb.tile([P, J], U32, align_bytes=64)
        kept_scales = sb.tile([P, J], U8, align_bytes=64)
        nc.vector.quantize_mx(out=kept_codes[:].bitcast(FP8X4), scales=kept_scales[:], in_=kept_bf[:].rearrange("p j t -> p (j t)"))
        key_codes = sb.tile([P, I], U32, align_bytes=64)
        for h in range(2):
            entries = slot_list[:, h * HALF // LIST_ROWS : (h + 1) * HALF // LIST_ROWS]
            nc.vector.tensor_copy(key_codes[:, h * HALF : (h + 1) * HALF], word_pool[:].bitcast(U32).indirect(entries))

        query_bf = sb.tile([P, Q, PACK], BF16, align_bytes=64)
        nc.scalar.copy(query_bf[:], query_raw[:].rearrange("p t q -> p q t"))
        query_codes = sb.tile([P, Q], U32, align_bytes=64)
        query_scales = sb.tile([P, Q], U8, align_bytes=64)
        nc.vector.quantize_mx(out=query_codes[:].bitcast(FP8X4), scales=query_scales[:], in_=query_bf[:].rearrange("p q t -> p (q t)"))

        kw_turned = bank("val0", "kw_turned")
        nc.tensor.transpose(kw_turned[:, 0:P], kw_rows[:], ident[:])
        kw_cols = sb.tile([P, LAM_ROW + 1], F32)
        nc.scalar.copy(kw_cols[:], kw_turned[:, 0 : LAM_ROW + 1])
        lam_bank = bank("late", "lam_bank")
        nc.tensor.transpose(lam_bank[:, 0:P], kw_cols[:, LAM_ROW : LAM_ROW + 1].to_broadcast([P, P]), ident[:])
        lam_rows = sb.tile([P, Q], F32)
        nc.scalar.copy(lam_rows[:], lam_bank[:, 0:P])

        picked = [sb.tile([P, I], BF16, name=f"val_picked{b}") for b in range(E // P)]

        def turn(sources, turned):
            for b, source in enumerate(sources):
                words = source.bitcast(F32)
                for u in range(2):
                    at = (2 * b + u) * P
                    nc.tensor.transpose(turned[:, at : at + P], words[:, u : 2 * P : 2], ident[:])

        def weave(turned, count, dst_bf):
            nc.scalar.copy(
                dst_bf.bitcast(F32).rearrange("p (b r u) -> p b r u", b=count, u=2),
                turned[:, : 2 * count * P].rearrange("p (b u r) -> p b r u", b=count, u=2),
            )

        def gather_vals(b):
            nc.vector.tensor_copy(picked[b][:], val_pool[b][:].indirect(slot_list[:]))

        def turn_vals(lo, hi, tag):
            turned = bank(tag, f"val_turned{lo}")
            turn([picked[b][:] for b in range(lo, hi)], turned)
            return turned

        weighted0 = sb.tile([P, I], F32)
        pair_max = sb.tile([P, I], F32)
        for h, tags in enumerate((("kk0", "kk1"), ("val0", "val1"))):
            slots = slice(h * HALF, (h + 1) * HALF)
            kk = [bank(tag, f"kk{h}{c}") for c, tag in enumerate(tags)]
            for c in range(J // P):
                cols = slice(c * P, (c + 1) * P)
                nc.tensor.matmul_mx(
                    out=kk[c][:, :HALF], lhsT=kept_codes[:, cols].bitcast(FP8X4), lhsT_scale=kept_scales[:, cols],
                    rhs=key_codes[:, slots].bitcast(FP8X4), rhs_scale=key_scales[:, slots], start=True, stop=True,
                )
            nc.scalar.activation(weighted0[:, slots], kk[0][:, :HALF], ACT.Copy, scale=kw_cols[:, 0:1])
            nc.vector.scalar_tensor_tensor(pair_max[:, slots], kk[1][:, :HALF], kw_cols[:, 1:2], weighted0[:, slots], ALU.mult, ALU.max)

        a0 = bank("a0", "a0")
        for r in range(I // P):
            cols = slice(r * P, (r + 1) * P)
            nc.tensor.matmul_mx(
                out=a0[:, cols], lhsT=key_codes[:, cols].bitcast(FP8X4), lhsT_scale=key_scales[:, cols],
                rhs=query_codes[:].bitcast(FP8X4), rhs_scale=query_scales[:], start=True, stop=True,
            )
        a0_sb = sb.tile([P, I // P * Q], F32)
        nc.scalar.copy(a0_sb[:], a0[:])

        gather_vals(0)
        neg_m1 = sb.tile([P, I // P], F32, tag="val0", align_bytes=64)
        for h, tag in enumerate(("turn", "kk1")):
            max_turned = bank(tag, f"max_turned{h}")
            for r in range(2):
                at = h * HALF + r * P
                nc.tensor.transpose(max_turned[:, r * P : (r + 1) * P], pair_max[:, at : at + P], ident[:])
            nc.vector.tensor_reduce(
                neg_m1[:, 2 * h : 2 * h + 2], max_turned[:, :HALF].rearrange("p (r j) -> p r j", j=P), AXIS_X, ALU.max, negate=True
            )

        scores = bank("kk0", "scores")
        for r in range(I // P):
            cols = slice(r * P, (r + 1) * P)
            nc.tensor.matmul(scores[:, cols], a0_sb[:, cols], ident[:], start=(r == 0), stop=False, is_transpose=True)
        penalty = sb.tile([P, I // P * Q], F32)
        for r in range(I // P):
            cols = slice(r * P, (r + 1) * P)
            nc.scalar.activation(penalty[:, cols], lam_rows[:], ACT.Copy, scale=neg_m1[:, r : r + 1])
            nc.tensor.matmul(scores[:, cols], penalty[:, cols], ident[:], start=False, stop=(r == I // P - 1), is_transpose=True)

        os_turned = bank("late", "os_turned")
        nc.tensor.transpose(os_turned[:, 0:P], os_rows[:], ident[:])
        os_cols = sb.tile([P, I // P], F32, tag="val0", align_bytes=64)
        nc.scalar.copy(os_cols[:], os_turned[:, 0 : I // P])
        os_bank = bank("os", "os_bank")
        for c in range(I // P):
            nc.tensor.transpose(os_bank[:, c * P : (c + 1) * P], os_cols[:, c : c + 1].to_broadcast([P, P]), ident[:])

        gather_vals(1)
        first_turned = turn_vals(0, 2, "late")
        neg_max = sb.tile([P, 1], F32, tag="val1", align_bytes=64)
        nc.vector.tensor_reduce(neg_max[:], scores[:], AXIS_X, ALU.max, negate=True)
        probs = sb.tile([P, I], F32)
        row_sum = sb.tile([P, 1], F32)
        nc.scalar.activation(probs[:], scores[:], ACT.Exp, bias=neg_max[:], accum_out=row_sum[:])
        gather_vals(2)
        val_bf = sb.tile([P, E * PACK], BF16, tag="val1", align_bytes=64)
        weave(first_turned, 2, val_bf[:, 0 : 2 * P * PACK])
        inv_sum = sb.tile([P, 1], F32, tag="val2", align_bytes=64)
        nc.vector.reciprocal(inv_sum[:], row_sum[:])
        weights = sb.tile([P, I], BF16)
        nc.vector.scalar_tensor_tensor(weights[:], probs[:], inv_sum[:], os_bank[:], ALU.mult, ALU.mult)
        weave(turn_vals(2, 3, "val0"), 1, val_bf[:, 2 * P * PACK : 3 * P * PACK])
        gather_vals(3)
        weight_bf = sb.tile([P, Q * PACK], BF16, align_bytes=64)
        weights_turned = bank("kk1", "weights_turned")
        turn([weights[:]], weights_turned)
        weave(weights_turned, 1, weight_bf[:])
        weave(turn_vals(3, 4, "val1"), 1, val_bf[:, 3 * P * PACK :])

        codes = sb.tile([P, Q + E], U32, tag="val3", align_bytes=64)
        scales = sb.tile([P, Q + E], U8, align_bytes=64)

        def quantise_vals(lo, hi):
            nc.vector.quantize_mx(
                out=codes[:, Q + lo : Q + hi].bitcast(FP8X4), scales=scales[:, Q + lo : Q + hi], in_=val_bf[:, lo * PACK : hi * PACK]
            )

        def product(dst, lo, hi):
            nc.tensor.matmul_mx(
                out=dst, lhsT=codes[:, :Q].bitcast(FP8X4), lhsT_scale=scales[:, :Q],
                rhs=codes[:, Q + lo : Q + hi].bitcast(FP8X4), rhs_scale=scales[:, Q + lo : Q + hi], start=True, stop=True,
            )

        quantise_vals(0, 2 * P)
        nc.vector.quantize_mx(out=codes[:, :Q].bitcast(FP8X4), scales=scales[:, :Q], in_=weight_bf[:])
        quantise_vals(2 * P, EARLY)
        early = bank("a0", "out_early")
        product(early[:, 0 : 2 * P], 0, 2 * P)
        product(early[:, 2 * P : EARLY], 2 * P, EARLY)
        early_sb = sb.tile([P, EARLY], F32)
        nc.scalar.copy(early_sb[:], early[:, 0:EARLY])
        nc.sync.dma_start(out[:, 0:EARLY], early_sb[:])

        quantise_vals(EARLY, E)
        late = bank("late", "out_late")
        product(late[:, 0 : E - EARLY], EARLY, E)
        late_sb = sb.tile([P, E - EARLY], F32)
        nc.vector.tensor_copy(late_sb[:], late[:, 0 : E - EARLY])
        nc.sync.dma_start(out[:, EARLY:E], late_sb[:])
